import numpy as np
import ml_dtypes


def mxq(x, axis, fmt="e4m3"):
    dtype, down = {"e4m3": (ml_dtypes.float8_e4m3fn, 7), "e5m2": (ml_dtypes.float8_e5m2, 14)}[fmt]
    v = np.moveaxis(np.asarray(x, np.float32).astype(ml_dtypes.bfloat16).astype(np.float64), axis, -1)
    blocks = v.reshape(v.shape[:-1] + (-1, 32))
    amax = np.abs(blocks).max(-1, keepdims=True)
    byte = np.maximum(np.where(amax > 0, np.frexp(amax)[1] - 1 + 127, 0) - down, 1)
    scale = np.exp2(byte - 127.0)
    codes = (blocks / scale).astype(np.float32).astype(dtype).astype(np.float64)
    return np.moveaxis((codes * scale).reshape(v.shape), -1, axis)


WIDE = False


def mx_kscale(k):
    if not WIDE:
        return np.ones(k)
    levels = np.array([10, -10, 5, -5, 0])
    if k % 512:
        return np.exp2(np.random.permutation(np.resize(levels, k // 32))).repeat(32)
    a = np.empty((k // 512, 16))
    for p in range(k // 512):
        a[p, :8] = np.random.permutation(np.resize(levels, 8))
        for g in range(8):
            far = levels[np.abs(levels - a[p, g]) >= 10]
            a[p, g + 8] = far[np.random.randint(len(far))]
    return np.exp2(a.ravel()).repeat(32)


BF16 = ml_dtypes.bfloat16


def bf(x):
    return np.asarray(x, np.float32).astype(BF16)


def f64(x):
    return np.asarray(x).astype(np.float64)


E, K, D, C, NB = 256, 16, 512, 128, 8
NBC = NB * C


def silu(v):
    return v / (1.0 + np.exp(-v))


def draw0():
    s = mx_kscale(D)
    t = mx_kscale(NBC)
    m_kj = bf(np.random.standard_normal((E, K, D)) * s)
    m_ji = bf(np.random.standard_normal((E, D)))
    sbf = bf(np.random.standard_normal((E, K, NB)))
    w_down = bf(np.random.standard_normal((D, C)) / np.sqrt(D) / s[:, None])
    gain = bf((1.0 + 0.1 * np.random.standard_normal(NBC)) * t)
    w_bil = bf(np.random.standard_normal((NBC, D)) * 2.0 / np.sqrt(NBC) / t[:, None])
    return {"m_kj": m_kj, "m_ji": m_ji, "sbf": sbf, "w_down": w_down, "gain": gain, "w_bil": w_bil}


def core(m_kj, m_ji, sbf, w_down, gain, w_bil):
    m_kj, m_ji, sbf, w_down, gain, w_bil = f64(m_kj), f64(m_ji), f64(sbf), f64(w_down), f64(gain), f64(w_bil)
    e, k, _ = m_kj.shape
    nbc = gain.shape[0]
    x = silu(mxq(m_kj, 2, "e4m3") @ mxq(w_down, 0, "e4m3"))
    q = (sbf[:, :, :, None] * x[:, :, None, :]).reshape(e, k, nbc)
    p = q * gain
    t = silu(mxq(p, 2, "e4m3") @ mxq(w_bil, 0, "e4m3"))
    agg = np.sum(t, axis=1) / np.sqrt(k)
    return m_ji + agg


def e4m3fn_bytes(y):
    return np.clip(np.asarray(y, np.float64), -448.0, 448.0).astype(np.float32).astype(ml_dtypes.float8_e4m3fn).view(np.uint8)


def e4m3fn_values(b):
    return np.asarray(b, np.uint8).view(ml_dtypes.float8_e4m3fn).astype(np.float64)


def setup_inputs():
    d = draw0()
    x0 = np.asarray(d['m_kj']).astype(np.float64)
    s = (np.max(np.abs(x0), axis=(0, 1), keepdims=True) / 448.0).astype(np.float32)
    out = {}
    for k, v in d.items():
        if k == 'm_kj':
            out['m_kj_bytes'] = e4m3fn_bytes(x0 / s.astype(np.float64))
            out['m_kj_scale'] = s
        else:
            out[k] = v
    return out


def reference(m_kj_bytes, m_kj_scale, m_ji, sbf, w_down, gain, w_bil):
    return core(e4m3fn_values(m_kj_bytes) * m_kj_scale.astype(np.float64), m_ji, sbf, w_down, gain, w_bil)

@@ -1,0 +1,248 @@
+from contextlib import ExitStack
+
+import concourse.mybir as mybir
+from concourse.masks import make_identity
+
+E, K, D, C, NB = 256, 16, 512, 128, 8
+NBC = NB * C
+P = 128
+FLOPS = 2 * E * K * D * C + 2 * E * K * NBC * D
+
+F32 = mybir.dt.float32
+BF16 = mybir.dt.bfloat16
+U32 = mybir.dt.uint32
+U8 = mybir.dt.uint8
+FP8 = mybir.dt.float8_e4m3fn
+FP8X4 = mybir.dt.float8_e4m3fn_x4
+MULT = mybir.AluOpType.mult
+ADD = mybir.AluOpType.add
+SILU = mybir.ActivationFunctionType.Silu
+
+TILES = 32
+GT = 4
+GROUPS = TILES // GT
+
+
+def tile_dimenettripletbilinear_kernel(tc, m_kj_bytes, m_kj_scale, m_ji, sbf, w_down, gain, w_bil, out):
+    nc = tc.nc
+    with ExitStack() as ctx:
+        const = ctx.enter_context(tc.tile_pool(name="const", bufs=1))
+        work = ctx.enter_context(tc.tile_pool(name="work", bufs=2))
+        psum = ctx.enter_context(tc.psum_pool(name="psum", bufs=1))
+        ctx.enter_context(tc.manual_schedule())
+
+        scale_bc = const.tile([P, D], F32, name="scale_bc", align_bytes=64)
+        nc.sync.dma_start(out=scale_bc[:], in_=m_kj_scale.rearrange("a b k -> (a b k)").partition_broadcast(P))
+        bytes_hbm = m_kj_bytes.rearrange("(h e) (q j) k -> h q e (j k)", e=P, j=GT)
+        mbytes = []
+
+        def load_bytes(s):
+            t = const.tile([P, GT * D], U8, name="mbytes%d" % s, align_bytes=64)
+            nc.sync.dma_start(out=t[:], in_=bytes_hbm[s // 4, s % 4])
+            mbytes.append(t)
+
+        load_bytes(0)
+        wd_raw = const.tile([P, 4, C], BF16, name="wd_raw", align_bytes=64)
+        nc.sync.dma_start(out=wd_raw[:], in_=w_down.rearrange("(p j) c -> p j c", j=4))
+        g_raw = const.tile([1, NBC], BF16, name="g_raw", align_bytes=64)
+        nc.sync.dma_start(out=g_raw[:], in_=gain.unsqueeze(0))
+        sbf_raw = const.tile([P, 2, K * NB], BF16, name="sbf_raw", align_bytes=64)
+        nc.sync.dma_start(out=sbf_raw[:], in_=sbf.rearrange("(h e) k n -> e h (k n)", e=P))
+        load_bytes(1)
+        load_bytes(2)
+        wb_raw = const.tile([P, 2, 4, D], BF16, name="wb_raw", align_bytes=64)
+        wb_hbm = w_bil.rearrange("(g p j) d -> g p j d", g=2, j=4)
+        for g in range(2):
+            nc.sync.dma_start(out=wb_raw[:, g], in_=wb_hbm[g])
+        for s in range(3, GROUPS):
+            load_bytes(s)
+        mji = const.tile([P, 2, D], BF16, name="mji", align_bytes=64)
+        nc.sync.dma_start(out=mji[:], in_=m_ji.rearrange("(h e) d -> e h d", e=P))
+
+        warm = const.tile([P, 1], F32, name="warm")
+        nc.vector.memset(warm[:], 0.0)
+        warm2 = const.tile([P, 1], F32, name="warm2")
+        nc.scalar.activation(out=warm2[:], in_=warm[:], func=SILU)
+        ident = const.tile([P, P], F32, name="ident", align_bytes=64)
+        make_identity(nc, ident[:])
+        ones = const.tile([P, P], BF16, name="ones", align_bytes=64)
+        nc.gpsimd.memset(ones[:], 1.0)
+        g_zero = const.tile([P, NBC], BF16, name="g_zero", align_bytes=64)
+        nc.gpsimd.memset(g_zero[:], 0.0)
+        for u in range(2):
+            nc.gpsimd.tensor_copy(
+                out=g_zero[0:1, :].rearrange("o (n u i e) -> o u n i e", u=2, i=32, e=2)[:, u],
+                in_=g_raw[:].rearrange("o (n i u e) -> o u n i e", u=2, i=32, e=2)[:, u],
+            )
+        sbf_f = const.tile([P, 2 * K * NB], F32, name="sbf_f", align_bytes=64)
+        nc.gpsimd.tensor_copy(out=sbf_f[:], in_=sbf_raw[:].rearrange("p h k -> p (h k)"))
+
+        wd_grp = const.tile([P, C, 4], BF16, name="wd_grp", align_bytes=64)
+        for u in range(2):
+            nc.vector.tensor_copy(
+                out=wd_grp[:].rearrange("p (u i e) j -> p u i e j", u=2, e=2)[:, u],
+                in_=wd_raw[:].rearrange("p j (i u e) -> p u i e j", u=2, e=2)[:, u],
+            )
+        wd_codes = const.tile([P, C], U32, name="wd_codes", align_bytes=64)
+        wd_sc = const.tile([P, C], U8, name="wd_sc", align_bytes=64)
+        nc.vector.quantize_mx(out=wd_codes[:].bitcast(FP8X4), scales=wd_sc[:], in_=wd_grp[:].rearrange("p c j -> p (c j)"))
+
+        wb_grp = const.tile([P, 2, D, 4], BF16, name="wb_grp", align_bytes=64)
+        wb_codes = const.tile([P, 2, D], U32, name="wb_codes", align_bytes=64)
+        wb_sc = const.tile([P, 2, D], U8, name="wb_sc", align_bytes=64)
+
+        gain_ps = psum.tile([P, NBC], BF16, name="gain_ps")
+        for a in range(2):
+            nc.tensor.matmul(out=gain_ps[:, a * 512:(a + 1) * 512], lhsT=ones[:], rhs=g_zero[:, a * 512:(a + 1) * 512], start=True, stop=True)
+
+        mw, mtr, mq, mcode, yps, xs, pts, ptr, pqs, pcode, mm, tts, aggs = {}, {}, {}, {}, {}, {}, {}, {}, {}, {}, {}, {}, {}
+
+        def product(t):
+            mw_t = work.tile([P, D], BF16, name="mw", bufs=6, align_bytes=64)
+            nc.vector.tensor_tensor(
+                out=mw_t[:], in0=mbytes[t // GT][:, (t % GT) * D:(t % GT + 1) * D].bitcast(FP8), in1=scale_bc[:], op=MULT
+            )
+            mw[t] = mw_t
+
+        def m_transpose(s, b):
+            tr_t = psum.tile([P, 2, 2, P], F32, name="tr", bufs=3)
+            for j in range(2):
+                words = mw[GT * s + 2 * b + j][:].bitcast(F32)
+                for u in range(2):
+                    nc.tensor.transpose(tr_t[:, j, u, :], words[:, u:256:2], ident[:])
+            mtr[s, b] = tr_t
+
+        def m_copy(s, b):
+            if b == 0:
+                mq_t = work.tile([P, GT * P * 4], BF16, name="mq", bufs=2, align_bytes=64)
+                mq[s] = mq_t
+            dst = mq[s][:].bitcast(F32)[:, b * 512:(b + 1) * 512].rearrange("p (j r u) -> p j r u", j=2, u=2)
+            nc.scalar.copy(out=dst, in_=mtr[s, b][:].rearrange("p j u r -> p j r u"))
+
+        def m_quant(s):
+            mc_t = work.tile([P, GT * P], U32, name="mc", bufs=2, align_bytes=64)
+            ms_t = work.tile([P, GT * P], U8, name="ms", bufs=2, align_bytes=64)
+            nc.vector.quantize_mx(out=mc_t[:].bitcast(FP8X4), scales=ms_t[:], in_=mq[s][:])
+            mcode[s] = (mc_t, ms_t)
+
+        def stage1(s):
+            y_t = psum.tile([P, GT, C], F32, name="y", bufs=1)
+            mc_t, ms_t = mcode[s]
+            for j in range(GT):
+                cols = slice(j * P, (j + 1) * P)
+                nc.tensor.matmul_mx(
+                    out=y_t[:, j, :], lhsT=mc_t[:, cols].bitcast(FP8X4), lhsT_scale=ms_t[:, cols],
+                    rhs=wd_codes[:].bitcast(FP8X4), rhs_scale=wd_sc[:], start=True, stop=True,
+                )
+            yps[s] = y_t
+
+        def silu1(s):
+            x_t = work.tile([P, GT, C], F32, name="x", bufs=2, align_bytes=64)
+            nc.scalar.activation(out=x_t[:], in_=yps[s][:], func=SILU)
+            xs[s] = x_t
+
+        def p_ops(t):
+            s, j = t // GT, t % GT
+            p_t = work.tile([P, NBC], BF16, name="pt", bufs=3, align_bytes=64)
+            view = p_t[:].rearrange("p (g u n w) -> p g u n w", g=2, u=2, n=4)
+            for n in range(NB):
+                col = t * NB + n
+                nc.vector.scalar_tensor_tensor(
+                    out=view[:, n // 4, :, n % 4, :],
+                    in0=xs[s][:, j, :].rearrange("p (u w) -> p u w", u=2),
+                    scalar=sbf_f[:, col:col + 1],
+                    in1=gain_ps[:, n * C:(n + 1) * C].rearrange("p (u w) -> p u w", u=2),
+                    op0=MULT, op1=MULT,
+                )
+            pts[t] = p_t
+
+        def p_transpose(t):
+            tr_t = psum.tile([P, 4, P], F32, name="tr", bufs=3)
+            words = pts[t][:].bitcast(F32)
+            for a in range(4):
+                nc.tensor.transpose(tr_t[:, a, :], words[:, a * P:(a + 1) * P], ident[:])
+            ptr[t] = tr_t
+
+        def p_copy(t):
+            s, j = t // GT, t % GT
+            if j == 0:
+                pq_t = work.tile([P, 2, GT * P * 4], BF16, name="pq", bufs=2, align_bytes=64)
+                pqs[s] = pq_t
+            dst = pqs[s][:].bitcast(F32).rearrange("p g (j r u) -> p g j r u", j=GT, u=2)[:, :, j]
+            nc.scalar.copy(out=dst, in_=ptr[t][:].rearrange("p (g u) r -> p g r u", g=2))
+
+        def p_quant(s):
+            pc_t = work.tile([P, 2, GT * P], U32, name="pc", bufs=2, align_bytes=64)
+            ps_t = work.tile([P, 2, GT * P], U8, name="ps", bufs=2, align_bytes=64)
+            for g in range(2):
+                nc.vector.quantize_mx(out=pc_t[:, g, :].bitcast(FP8X4), scales=ps_t[:, g, :], in_=pqs[s][:, g, :])
+            pcode[s] = (pc_t, ps_t)
+
+        def stage2(s, d):
+            mm_t = psum.tile([P, GT * P], F32, name="mm", bufs=2)
+            pc_t, ps_t = pcode[s]
+            cols = slice(d * P, (d + 1) * P)
+            for g in range(2):
+                nc.tensor.matmul_mx(
+                    out=mm_t[:], lhsT=wb_codes[:, g, cols].bitcast(FP8X4), lhsT_scale=wb_sc[:, g, cols],
+                    rhs=pc_t[:, g, :].bitcast(FP8X4), rhs_scale=ps_t[:, g, :], start=(g == 0), stop=(g == 1),
+                )
+            mm[s, d] = mm_t
+
+        def silu2(s, d):
+            t_t = work.tile([P, GT * P], F32, name="tt", bufs=4, align_bytes=64)
+            nc.scalar.activation(out=t_t[:], in_=mm[s, d][:], func=SILU)
+            tts[s, d] = t_t
+
+        def k_sum(s, d):
+            h = s // 4
+            if s % 4 == 0 and d == 0:
+                agg_t = psum.tile([P, D], F32, name="agg", bufs=1)
+                aggs[h] = agg_t
+            for j in range(GT):
+                nc.tensor.matmul(
+                    out=aggs[h][:, d * P:(d + 1) * P], lhsT=tts[s, d][:, j * P:(j + 1) * P], rhs=ident[:], is_transpose=True,
+                    start=(s % 4 == 0 and d == 0 and j == 0), stop=(s % 4 == 3 and d == 3 and j == GT - 1),
+                )
+            if s % 4 == 3 and d == 3:
+                o_t = work.tile([P, D], F32, name="o", bufs=2, align_bytes=64)
+                nc.vector.scalar_tensor_tensor(out=o_t[:], in0=aggs[h][:], scalar=0.25, in1=mji[:, h, :], op0=MULT, op1=ADD)
+                nc.sync.dma_start(out=out[h * P:(h + 1) * P, :], in_=o_t[:])
+
+        def wb_group(a):
+            g, half = a // 2, a % 2
+            d = slice(half * 256, half * 256 + 256)
+            nc.scalar.copy(out=wb_grp[:, g, d, :], in_=wb_raw[:, g, :, d].rearrange("p j d -> p d j"))
+
+        for q in range(-7, TILES + 6):
+            if 0 <= q < TILES:
+                p_ops(q)
+            if (q + 2) % GT == 0 and 0 <= (q + 2) // GT < GROUPS:
+                m_quant((q + 2) // GT)
+            if q == 3:
+                for g in range(2):
+                    nc.vector.quantize_mx(out=wb_codes[:, g, :].bitcast(FP8X4), scales=wb_sc[:, g, :], in_=wb_grp[:, g].rearrange("p d j -> p (d j)"))
+            if 0 <= q - 5 < TILES:
+                stage2((q - 5) // GT, (q - 5) % GT)
+            if (q + 2) % GT == 0 and 0 <= (q + 2) // GT < GROUPS:
+                stage1((q + 2) // GT)
+            if 0 <= q - 1 < TILES:
+                p_transpose(q - 1)
+            if 0 <= q - 6 < TILES:
+                k_sum((q - 6) // GT, (q - 6) % GT)
+            if q % GT in (0, 1) and 0 <= q // GT + 1 < GROUPS:
+                m_transpose(q // GT + 1, q % GT)
+            if 0 <= q - 1 < TILES:
+                p_copy(q - 1)
+            if (q + 2) % GT == 0 and 0 <= (q + 2) // GT < GROUPS:
+                silu1((q + 2) // GT)
+            if 0 <= q - 5 < TILES:
+                silu2((q - 5) // GT, (q - 5) % GT)
+            if q % GT in (0, 1) and 0 <= q // GT + 1 < GROUPS:
+                m_copy(q // GT + 1, q % GT)
+            if 0 <= q + 1 < 4:
+                wb_group(q + 1)
+            if q % GT == 0 and 1 <= q // GT <= GROUPS:
+                p_quant(q // GT - 1)
+            if 0 <= q + 7 < TILES:
+                product(q + 7)

@@ -19,8 +19,10 @@ ADD = mybir.AluOpType.add
 SILU = mybir.ActivationFunctionType.Silu
 
 TILES = 32
-GT = 4
-GROUPS = TILES // GT
+HALF = 16
+M_CHUNKS = [[0], [1]] + [[t, t + 1] for t in range(2, TILES, 2)]
+P_CHUNKS = [[t, t + 1] for t in range(0, TILES - 2, 2)] + [[TILES - 2], [TILES - 1]]
+LOADS = [(0, 2), (2, 4), (4, 8), (8, 12), (12, 16), (16, 20), (20, 24), (24, 28), (28, 32)]
 
 
 def tile_dimenettripletbilinear_kernel(tc, m_kj_bytes, m_kj_scale, m_ji, sbf, w_down, gain, w_bil, out):
@@ -31,31 +33,34 @@ def tile_dimenettripletbilinear_kernel(tc, m_kj_bytes, m_kj_scale, m_ji, sbf, w_
         psum = ctx.enter_context(tc.psum_pool(name="psum", bufs=1))
         ctx.enter_context(tc.manual_schedule())
 
+        mbytes = {}
+
+        def load_bytes(t0, t1):
+            t_t = const.tile([P, (t1 - t0) * D], U8, name="mbytes%d" % t0, align_bytes=64)
+            h = t0 // HALF
+            nc.sync.dma_start(
+                out=t_t[:], in_=m_kj_bytes[h * P:(h + 1) * P, t0 - h * HALF:t1 - h * HALF, :].rearrange("e k d -> e (k d)")
+            )
+            for t in range(t0, t1):
+                mbytes[t] = t_t[:, (t - t0) * D:(t - t0 + 1) * D]
+
         scale_bc = const.tile([P, D], F32, name="scale_bc", align_bytes=64)
         nc.sync.dma_start(out=scale_bc[:], in_=m_kj_scale.rearrange("a b k -> (a b k)").partition_broadcast(P))
-        bytes_hbm = m_kj_bytes.rearrange("(h e) (q j) k -> h q e (j k)", e=P, j=GT)
-        mbytes = []
-
-        def load_bytes(s):
-            t = const.tile([P, GT * D], U8, name="mbytes%d" % s, align_bytes=64)
-            nc.sync.dma_start(out=t[:], in_=bytes_hbm[s // 4, s % 4])
-            mbytes.append(t)
-
-        load_bytes(0)
+        load_bytes(*LOADS[0])
         wd_raw = const.tile([P, 4, C], BF16, name="wd_raw", align_bytes=64)
         nc.sync.dma_start(out=wd_raw[:], in_=w_down.rearrange("(p j) c -> p j c", j=4))
         g_raw = const.tile([1, NBC], BF16, name="g_raw", align_bytes=64)
         nc.sync.dma_start(out=g_raw[:], in_=gain.unsqueeze(0))
         sbf_raw = const.tile([P, 2, K * NB], BF16, name="sbf_raw", align_bytes=64)
         nc.sync.dma_start(out=sbf_raw[:], in_=sbf.rearrange("(h e) k n -> e h (k n)", e=P))
-        load_bytes(1)
-        load_bytes(2)
+        load_bytes(*LOADS[1])
+        load_bytes(*LOADS[2])
         wb_raw = const.tile([P, 2, 4, D], BF16, name="wb_raw", align_bytes=64)
         wb_hbm = w_bil.rearrange("(g p j) d -> g p j d", g=2, j=4)
         for g in range(2):
             nc.sync.dma_start(out=wb_raw[:, g], in_=wb_hbm[g])
-        for s in range(3, GROUPS):
-            load_bytes(s)
+        for t0, t1 in LOADS[3:]:
+            load_bytes(t0, t1)
         mji = const.tile([P, 2, D], BF16, name="mji", align_bytes=64)
         nc.sync.dma_start(out=mji[:], in_=m_ji.rearrange("(h e) d -> e h d", e=P))
 
@@ -78,83 +83,98 @@ def tile_dimenettripletbilinear_kernel(tc, m_kj_bytes, m_kj_scale, m_ji, sbf, w_
         nc.gpsimd.tensor_copy(out=sbf_f[:], in_=sbf_raw[:].rearrange("p h k -> p (h k)"))
 
         wd_grp = const.tile([P, C, 4], BF16, name="wd_grp", align_bytes=64)
-        for u in range(2):
-            nc.vector.tensor_copy(
-                out=wd_grp[:].rearrange("p (u i e) j -> p u i e j", u=2, e=2)[:, u],
-                in_=wd_raw[:].rearrange("p j (i u e) -> p u i e j", u=2, e=2)[:, u],
-            )
         wd_codes = const.tile([P, C], U32, name="wd_codes", align_bytes=64)
         wd_sc = const.tile([P, C], U8, name="wd_sc", align_bytes=64)
-        nc.vector.quantize_mx(out=wd_codes[:].bitcast(FP8X4), scales=wd_sc[:], in_=wd_grp[:].rearrange("p c j -> p (c j)"))
+
+        def wd_prepare():
+            for u in range(2):
+                nc.vector.tensor_copy(
+                    out=wd_grp[:].rearrange("p (u i e) j -> p u i e j", u=2, e=2)[:, u],
+                    in_=wd_raw[:].rearrange("p j (i u e) -> p u i e j", u=2, e=2)[:, u],
+                )
+            nc.vector.quantize_mx(out=wd_codes[:].bitcast(FP8X4), scales=wd_sc[:], in_=wd_grp[:].rearrange("p c j -> p (c j)"))
 
         wb_grp = const.tile([P, 2, D, 4], BF16, name="wb_grp", align_bytes=64)
         wb_codes = const.tile([P, 2, D], U32, name="wb_codes", align_bytes=64)
         wb_sc = const.tile([P, 2, D], U8, name="wb_sc", align_bytes=64)
 
+        def wb_interleave(a):
+            g, half = a // 2, a % 2
+            d = slice(half * 256, half * 256 + 256)
+            nc.scalar.copy(out=wb_grp[:, g, d, :], in_=wb_raw[:, g, :, d].rearrange("p j d -> p d j"))
+
+        def wb_quantise(g):
+            nc.vector.quantize_mx(out=wb_codes[:, g, :].bitcast(FP8X4), scales=wb_sc[:, g, :], in_=wb_grp[:, g].rearrange("p d j -> p (d j)"))
+
         gain_ps = psum.tile([P, NBC], BF16, name="gain_ps")
-        for a in range(2):
-            nc.tensor.matmul(out=gain_ps[:, a * 512:(a + 1) * 512], lhsT=ones[:], rhs=g_zero[:, a * 512:(a + 1) * 512], start=True, stop=True)
+
+        def gain_spread():
+            for a in range(2):
+                nc.tensor.matmul(out=gain_ps[:, a * 512:(a + 1) * 512], lhsT=ones[:], rhs=g_zero[:, a * 512:(a + 1) * 512], start=True, stop=True)
 
         mw, mtr, mq, mcode, yps, xs, pts, ptr, pqs, pcode, mm, tts, aggs = {}, {}, {}, {}, {}, {}, {}, {}, {}, {}, {}, {}, {}
 
         def product(t):
             mw_t = work.tile([P, D], BF16, name="mw", bufs=6, align_bytes=64)
-            nc.vector.tensor_tensor(
-                out=mw_t[:], in0=mbytes[t // GT][:, (t % GT) * D:(t % GT + 1) * D].bitcast(FP8), in1=scale_bc[:], op=MULT
-            )
+            nc.vector.tensor_tensor(out=mw_t[:], in0=mbytes[t].bitcast(FP8), in1=scale_bc[:], op=MULT)
             mw[t] = mw_t
 
-        def m_transpose(s, b):
+        def m_transpose(c):
             tr_t = psum.tile([P, 2, 2, P], F32, name="tr", bufs=3)
-            for j in range(2):
-                words = mw[GT * s + 2 * b + j][:].bitcast(F32)
+            for j, t in enumerate(M_CHUNKS[c]):
+                words = mw[t][:].bitcast(F32)
                 for u in range(2):
                     nc.tensor.transpose(tr_t[:, j, u, :], words[:, u:256:2], ident[:])
-            mtr[s, b] = tr_t
+            mtr[c] = tr_t
 
-        def m_copy(s, b):
-            if b == 0:
-                mq_t = work.tile([P, GT * P * 4], BF16, name="mq", bufs=2, align_bytes=64)
-                mq[s] = mq_t
-            dst = mq[s][:].bitcast(F32)[:, b * 512:(b + 1) * 512].rearrange("p (j r u) -> p j r u", j=2, u=2)
-            nc.scalar.copy(out=dst, in_=mtr[s, b][:].rearrange("p j u r -> p j r u"))
+        def m_copy(c):
+            n = len(M_CHUNKS[c])
+            mq_t = work.tile([P, 2 * P * 4], BF16, name="mq", bufs=3, align_bytes=64)
+            dst = mq_t[:].bitcast(F32)[:, 0:n * 256].rearrange("p (j r u) -> p j r u", j=n, u=2)
+            nc.scalar.copy(out=dst, in_=mtr[c][:, 0:n].rearrange("p j u r -> p j r u"))
+            mq[c] = mq_t
 
-        def m_quant(s):
-            mc_t = work.tile([P, GT * P], U32, name="mc", bufs=2, align_bytes=64)
-            ms_t = work.tile([P, GT * P], U8, name="ms", bufs=2, align_bytes=64)
-            nc.vector.quantize_mx(out=mc_t[:].bitcast(FP8X4), scales=ms_t[:], in_=mq[s][:])
-            mcode[s] = (mc_t, ms_t)
+        def m_quant(c):
+            n = len(M_CHUNKS[c])
+            mc_t = work.tile([P, 2 * P], U32, name="mc", bufs=3, align_bytes=64)
+            ms_t = work.tile([P, 2 * P], U8, name="ms", bufs=3, align_bytes=64)
+            nc.vector.quantize_mx(out=mc_t[:, 0:n * P].bitcast(FP8X4), scales=ms_t[:, 0:n * P], in_=mq[c][:, 0:n * P * 4])
+            mcode[c] = (mc_t, ms_t)
 
-        def stage1(s):
-            y_t = psum.tile([P, GT, C], F32, name="y", bufs=1)
-            mc_t, ms_t = mcode[s]
-            for j in range(GT):
+        def stage1(c):
+            y_t = psum.tile([P, 2, C], F32, name="y", bufs=1)
+            mc_t, ms_t = mcode[c]
+            for j in range(len(M_CHUNKS[c])):
                 cols = slice(j * P, (j + 1) * P)
                 nc.tensor.matmul_mx(
                     out=y_t[:, j, :], lhsT=mc_t[:, cols].bitcast(FP8X4), lhsT_scale=ms_t[:, cols],
                     rhs=wd_codes[:].bitcast(FP8X4), rhs_scale=wd_sc[:], start=True, stop=True,
                 )
-            yps[s] = y_t
+            yps[c] = y_t
 
-        def silu1(s):
-            x_t = work.tile([P, GT, C], F32, name="x", bufs=2, align_bytes=64)
-            nc.scalar.activation(out=x_t[:], in_=yps[s][:], func=SILU)
-            xs[s] = x_t
+        def silu1(c):
+            n = len(M_CHUNKS[c])
+            x_t = work.tile([P, 2, C], F32, name="x", bufs=3, align_bytes=64)
+            nc.scalar.activation(out=x_t[:, 0:n], in_=yps[c][:, 0:n], func=SILU)
+            for j, t in enumerate(M_CHUNKS[c]):
+                xs[t] = x_t[:, j, :].rearrange("p (u w) -> p u w", u=2)
 
-        def p_ops(t):
-            s, j = t // GT, t % GT
-            p_t = work.tile([P, NBC], BF16, name="pt", bufs=3, align_bytes=64)
-            view = p_t[:].rearrange("p (g u n w) -> p g u n w", g=2, u=2, n=4)
-            for n in range(NB):
+        def p_ops(t, n0, n1):
+            if n0 == 0:
+                p_t = work.tile([P, NBC], BF16, name="pt", bufs=3, align_bytes=64)
+                pts[t] = p_t
+            view = pts[t][:].rearrange("p (g u n w) -> p g u n w", g=2, u=2, n=4)
+            for n in range(n0, n1):
                 col = t * NB + n
                 nc.vector.scalar_tensor_tensor(
-                    out=view[:, n // 4, :, n % 4, :],
-                    in0=xs[s][:, j, :].rearrange("p (u w) -> p u w", u=2),
-                    scalar=sbf_f[:, col:col + 1],
-                    in1=gain_ps[:, n * C:(n + 1) * C].rearrange("p (u w) -> p u w", u=2),
-                    op0=MULT, op1=MULT,
+                    out=view[:, n // 4, :, n % 4, :], in0=xs[t], scalar=sbf_f[:, col:col + 1],
+                    in1=gain_ps[:, n * C:(n + 1) * C].rearrange("p (u w) -> p u w", u=2), op0=MULT, op1=MULT,
                 )
-            pts[t] = p_t
+
+        p_place = {}
+        for c, tiles in enumerate(P_CHUNKS):
+            for j, t in enumerate(tiles):
+                p_place[t] = (c, j)
 
         def p_transpose(t):
             tr_t = psum.tile([P, 4, P], F32, name="tr", bufs=3)
@@ -164,85 +184,127 @@ def tile_dimenettripletbilinear_kernel(tc, m_kj_bytes, m_kj_scale, m_ji, sbf, w_
             ptr[t] = tr_t
 
         def p_copy(t):
-            s, j = t // GT, t % GT
+            c, j = p_place[t]
+            n = len(P_CHUNKS[c])
             if j == 0:
-                pq_t = work.tile([P, 2, GT * P * 4], BF16, name="pq", bufs=2, align_bytes=64)
-                pqs[s] = pq_t
-            dst = pqs[s][:].bitcast(F32).rearrange("p g (j r u) -> p g j r u", j=GT, u=2)[:, :, j]
+                pq_t = work.tile([P, 2 * NBC], BF16, name="pq", bufs=3, align_bytes=64)
+                pqs[c] = pq_t
+            dst = pqs[c][:].bitcast(F32)[:, 0:n * 512].rearrange("p (g j r u) -> p g j r u", g=2, j=n, u=2)[:, :, j]
             nc.scalar.copy(out=dst, in_=ptr[t][:].rearrange("p (g u) r -> p g r u", g=2))
 
-        def p_quant(s):
-            pc_t = work.tile([P, 2, GT * P], U32, name="pc", bufs=2, align_bytes=64)
-            ps_t = work.tile([P, 2, GT * P], U8, name="ps", bufs=2, align_bytes=64)
-            for g in range(2):
-                nc.vector.quantize_mx(out=pc_t[:, g, :].bitcast(FP8X4), scales=ps_t[:, g, :], in_=pqs[s][:, g, :])
-            pcode[s] = (pc_t, ps_t)
+        def p_quant(c):
+            n = len(P_CHUNKS[c])
+            pc_t = work.tile([P, 4 * P], U32, name="pc", bufs=3, align_bytes=64)
+            ps_t = work.tile([P, 4 * P], U8, name="ps", bufs=3, align_bytes=64)
+            nc.vector.quantize_mx(out=pc_t[:, 0:2 * n * P].bitcast(FP8X4), scales=ps_t[:, 0:2 * n * P], in_=pqs[c][:, 0:n * NBC])
+            pcode[c] = (pc_t, ps_t)
 
-        def stage2(s, d):
-            mm_t = psum.tile([P, GT * P], F32, name="mm", bufs=2)
-            pc_t, ps_t = pcode[s]
-            cols = slice(d * P, (d + 1) * P)
-            for g in range(2):
-                nc.tensor.matmul_mx(
-                    out=mm_t[:], lhsT=wb_codes[:, g, cols].bitcast(FP8X4), lhsT_scale=wb_sc[:, g, cols],
-                    rhs=pc_t[:, g, :].bitcast(FP8X4), rhs_scale=ps_t[:, g, :], start=(g == 0), stop=(g == 1),
-                )
-            mm[s, d] = mm_t
+        def stage2(c, b):
+            n = len(P_CHUNKS[c])
+            per = 4 // n
+            mm_t = psum.tile([P, 4 * P], F32, name="mm", bufs=2)
+            pc_t, ps_t = pcode[c]
+            nc.tensor.matmul_mx(
+                out=mm_t[:], lhsT=wb_codes[:, 0, 0:P].bitcast(FP8X4), lhsT_scale=wb_sc[:, 0, 0:P],
+                rhs=wb_codes[:, 1, :].bitcast(FP8X4), rhs_scale=wb_sc[:, 1, :], start=True, stop=True,
+            )
+            for i in range(per):
+                d = b * per + i
+                cols = slice(d * P, (d + 1) * P)
+                for g in range(2):
+                    toks = slice(g * n * P, (g + 1) * n * P)
+                    nc.tensor.matmul_mx(
+                        out=mm_t[:, i * n * P:(i + 1) * n * P], lhsT=wb_codes[:, g, cols].bitcast(FP8X4), lhsT_scale=wb_sc[:, g, cols],
+                        rhs=pc_t[:, toks].bitcast(FP8X4), rhs_scale=ps_t[:, toks], start=(g == 0), stop=(g == 1),
+                    )
+            mm[c, b] = mm_t
 
-        def silu2(s, d):
-            t_t = work.tile([P, GT * P], F32, name="tt", bufs=4, align_bytes=64)
-            nc.scalar.activation(out=t_t[:], in_=mm[s, d][:], func=SILU)
-            tts[s, d] = t_t
+        def silu2(c, b):
+            t_t = work.tile([P, 4 * P], F32, name="tt", bufs=4, align_bytes=64)
+            nc.scalar.activation(out=t_t[:], in_=mm[c, b][:], func=SILU)
+            tts[c, b] = t_t
 
-        def k_sum(s, d):
-            h = s // 4
-            if s % 4 == 0 and d == 0:
+        def k_sum(c, b):
+            tiles = P_CHUNKS[c]
+            n = len(tiles)
+            per = 4 // n
+            h = tiles[0] // HALF
+            first = tiles[0] % HALF == 0 and b == 0
+            last = tiles[-1] % HALF == HALF - 1 and b == n - 1
+            if first:
                 agg_t = psum.tile([P, D], F32, name="agg", bufs=1)
                 aggs[h] = agg_t
-            for j in range(GT):
-                nc.tensor.matmul(
-                    out=aggs[h][:, d * P:(d + 1) * P], lhsT=tts[s, d][:, j * P:(j + 1) * P], rhs=ident[:], is_transpose=True,
-                    start=(s % 4 == 0 and d == 0 and j == 0), stop=(s % 4 == 3 and d == 3 and j == GT - 1),
-                )
-            if s % 4 == 3 and d == 3:
-                o_t = work.tile([P, D], F32, name="o", bufs=2, align_bytes=64)
-                nc.vector.scalar_tensor_tensor(out=o_t[:], in0=aggs[h][:], scalar=0.25, in1=mji[:, h, :], op0=MULT, op1=ADD)
-                nc.sync.dma_start(out=out[h * P:(h + 1) * P, :], in_=o_t[:])
+            for i in range(per):
+                d = b * per + i
+                for j in range(n):
+                    nc.tensor.matmul(
+                        out=aggs[h][:, d * P:(d + 1) * P], lhsT=tts[c, b][:, (i * n + j) * P:(i * n + j + 1) * P], rhs=ident[:],
+                        is_transpose=True, start=(first and i == 0 and j == 0), stop=(last and i == per - 1 and j == n - 1),
+                    )
+            return last
 
-        def wb_group(a):
-            g, half = a // 2, a % 2
-            d = slice(half * 256, half * 256 + 256)
-            nc.scalar.copy(out=wb_grp[:, g, d, :], in_=wb_raw[:, g, :, d].rearrange("p j d -> p d j"))
+        def finish(h):
+            o_t = work.tile([P, D], F32, name="o", bufs=2, align_bytes=64)
+            nc.vector.scalar_tensor_tensor(out=o_t[:], in0=aggs[h][:], scalar=0.25, in1=mji[:, h, :], op0=MULT, op1=ADD)
+            nc.sync.dma_start(out=out[h * P:(h + 1) * P, :], in_=o_t[:])
 
-        for q in range(-7, TILES + 6):
-            if 0 <= q < TILES:
-                p_ops(q)
-            if (q + 2) % GT == 0 and 0 <= (q + 2) // GT < GROUPS:
-                m_quant((q + 2) // GT)
-            if q == 3:
-                for g in range(2):
-                    nc.vector.quantize_mx(out=wb_codes[:, g, :].bitcast(FP8X4), scales=wb_sc[:, g, :], in_=wb_grp[:, g].rearrange("p d j -> p (d j)"))
-            if 0 <= q - 5 < TILES:
-                stage2((q - 5) // GT, (q - 5) % GT)
-            if (q + 2) % GT == 0 and 0 <= (q + 2) // GT < GROUPS:
-                stage1((q + 2) // GT)
+        quant_at, mm_at = {}, {}
+        for c, tiles in enumerate(P_CHUNKS):
+            t0 = tiles[0]
+            if t0 < TILES - 4:
+                quant_at.setdefault(t0 + 3, []).append(c)
+                for b in range(2):
+                    mm_at.setdefault(t0 + 4 + b, []).append((c, b))
+            else:
+                quant_at.setdefault(tiles[-1] + 1, []).append(c)
+        mm_at.setdefault(31, []).append((14, 0))
+        mm_at.setdefault(32, []).append((14, 1))
+        mm_at.setdefault(32, []).append((15, 0))
+        mm_at.setdefault(33, []).append((16, 0))
+
+        pending_silu, pending_sum = [], []
+        for q in range(-5, TILES + 4):
             if 0 <= q - 1 < TILES:
                 p_transpose(q - 1)
-            if 0 <= q - 6 < TILES:
-                k_sum((q - 6) // GT, (q - 6) % GT)
-            if q % GT in (0, 1) and 0 <= q // GT + 1 < GROUPS:
-                m_transpose(q // GT + 1, q % GT)
+            done = [P_CHUNKS[cb[0]][0] // HALF for cb in pending_sum if k_sum(*cb)]
+            pending_sum = []
+            for cb in pending_silu:
+                silu2(*cb)
+                pending_sum.append(cb)
+            pending_silu = []
             if 0 <= q - 1 < TILES:
                 p_copy(q - 1)
-            if (q + 2) % GT == 0 and 0 <= (q + 2) // GT < GROUPS:
-                silu1((q + 2) // GT)
-            if 0 <= q - 5 < TILES:
-                silu2((q - 5) // GT, (q - 5) % GT)
-            if q % GT in (0, 1) and 0 <= q // GT + 1 < GROUPS:
-                m_copy(q // GT + 1, q % GT)
+            if q == -2:
+                wd_prepare()
+            if 0 <= q < TILES:
+                p_ops(q, 0, 4)
+            for c in quant_at.get(q, []):
+                p_quant(c)
+            if 0 <= q < TILES:
+                p_ops(q, 4, 8)
+            for h in done:
+                finish(h)
+            if q == 3:
+                wb_quantise(0)
+                wb_quantise(1)
+            for c, tiles in enumerate(M_CHUNKS):
+                if q == tiles[0] - 2:
+                    m_quant(c)
+            if 0 <= q + 5 < TILES:
+                product(q + 5)
+            for c, tiles in enumerate(M_CHUNKS):
+                if q == tiles[0] - 3:
+                    m_transpose(c)
+                    m_copy(c)
+            for cb in mm_at.get(q, []):
+                stage2(*cb)
+                pending_silu.append(cb)
+            for c, tiles in enumerate(M_CHUNKS):
+                if q == tiles[0] - 2:
+                    stage1(c)
+                if q == tiles[0] - 1:
+                    silu1(c)
+            if q == -1:
+                gain_spread()
             if 0 <= q + 1 < 4:
-                wb_group(q + 1)
-            if q % GT == 0 and 1 <= q // GT <= GROUPS:
-                p_quant(q // GT - 1)
-            if 0 <= q + 7 < TILES:
-                product(q + 7)
+                wb_interleave(q + 1)

@@ -22,6 +22,9 @@ TILES = 32
 HALF = 16
 M_CHUNKS = [[0], [1]] + [[t, t + 1] for t in range(2, TILES, 2)]
 P_CHUNKS = [[t, t + 1] for t in range(0, TILES - 2, 2)] + [[TILES - 2], [TILES - 1]]
+V_CAST = [t for t in range(6, TILES) if t % 3 != 0]
+S_CAST = [t for t in range(8, TILES) if t % 3 == 0]
+OFFLOAD = V_CAST + S_CAST
 LOADS = [(0, 2), (2, 4), (4, 8), (8, 12), (12, 16), (16, 20), (20, 24), (24, 28), (28, 32)]
 
 
@@ -44,22 +47,21 @@ def tile_dimenettripletbilinear_kernel(tc, m_kj_bytes, m_kj_scale, m_ji, sbf, w_
             for t in range(t0, t1):
                 mbytes[t] = t_t[:, (t - t0) * D:(t - t0 + 1) * D]
 
+        g_raw = const.tile([1, NBC], BF16, name="g_raw", align_bytes=64)
+        nc.sync.dma_start(out=g_raw[:], in_=gain.unsqueeze(0))
         scale_bc = const.tile([P, D], F32, name="scale_bc", align_bytes=64)
         nc.sync.dma_start(out=scale_bc[:], in_=m_kj_scale.rearrange("a b k -> (a b k)").partition_broadcast(P))
         load_bytes(*LOADS[0])
         wd_raw = const.tile([P, 4, C], BF16, name="wd_raw", align_bytes=64)
         nc.sync.dma_start(out=wd_raw[:], in_=w_down.rearrange("(p j) c -> p j c", j=4))
-        g_raw = const.tile([1, NBC], BF16, name="g_raw", align_bytes=64)
-        nc.sync.dma_start(out=g_raw[:], in_=gain.unsqueeze(0))
         sbf_raw = const.tile([P, 2, K * NB], BF16, name="sbf_raw", align_bytes=64)
         nc.sync.dma_start(out=sbf_raw[:], in_=sbf.rearrange("(h e) k n -> e h (k n)", e=P))
         load_bytes(*LOADS[1])
-        load_bytes(*LOADS[2])
         wb_raw = const.tile([P, 2, 4, D], BF16, name="wb_raw", align_bytes=64)
         wb_hbm = w_bil.rearrange("(g p j) d -> g p j d", g=2, j=4)
         for g in range(2):
             nc.sync.dma_start(out=wb_raw[:, g], in_=wb_hbm[g])
-        for t0, t1 in LOADS[3:]:
+        for t0, t1 in LOADS[2:]:
             load_bytes(t0, t1)
         mji = const.tile([P, 2, D], BF16, name="mji", align_bytes=64)
         nc.sync.dma_start(out=mji[:], in_=m_ji.rearrange("(h e) d -> e h d", e=P))
@@ -75,12 +77,12 @@ def tile_dimenettripletbilinear_kernel(tc, m_kj_bytes, m_kj_scale, m_ji, sbf, w_
         g_zero = const.tile([P, NBC], BF16, name="g_zero", align_bytes=64)
         nc.gpsimd.memset(g_zero[:], 0.0)
         for u in range(2):
-            nc.gpsimd.tensor_copy(
+            nc.scalar.copy(
                 out=g_zero[0:1, :].rearrange("o (n u i e) -> o u n i e", u=2, i=32, e=2)[:, u],
                 in_=g_raw[:].rearrange("o (n i u e) -> o u n i e", u=2, i=32, e=2)[:, u],
             )
         sbf_f = const.tile([P, 2 * K * NB], F32, name="sbf_f", align_bytes=64)
-        nc.gpsimd.tensor_copy(out=sbf_f[:], in_=sbf_raw[:].rearrange("p h k -> p (h k)"))
+        nc.scalar.copy(out=sbf_f[:], in_=sbf_raw[:].rearrange("p h k -> p (h k)"))
 
         wd_grp = const.tile([P, C, 4], BF16, name="wd_grp", align_bytes=64)
         wd_codes = const.tile([P, C], U32, name="wd_codes", align_bytes=64)
@@ -99,8 +101,8 @@ def tile_dimenettripletbilinear_kernel(tc, m_kj_bytes, m_kj_scale, m_ji, sbf, w_
         wb_sc = const.tile([P, 2, D], U8, name="wb_sc", align_bytes=64)
 
         def wb_interleave(a):
-            g, half = a // 2, a % 2
-            d = slice(half * 256, half * 256 + 256)
+            g, part = a // 4, a % 4
+            d = slice(part * 128, part * 128 + 128)
             nc.scalar.copy(out=wb_grp[:, g, d, :], in_=wb_raw[:, g, :, d].rearrange("p j d -> p d j"))
 
         def wb_quantise(g):
@@ -115,8 +117,25 @@ def tile_dimenettripletbilinear_kernel(tc, m_kj_bytes, m_kj_scale, m_ji, sbf, w_
         mw, mtr, mq, mcode, yps, xs, pts, ptr, pqs, pcode, mm, tts, aggs = {}, {}, {}, {}, {}, {}, {}, {}, {}, {}, {}, {}, {}
 
         def product(t):
-            mw_t = work.tile([P, D], BF16, name="mw", bufs=6, align_bytes=64)
+            mw_t = work.tile([P, D], BF16, name="mw", bufs=8, align_bytes=64)
             nc.vector.tensor_tensor(out=mw_t[:], in0=mbytes[t].bitcast(FP8), in1=scale_bc[:], op=MULT)
+            mw[t] = mw_t
+
+        casts = {}
+
+        def product_cast(t):
+            c_t = work.tile([P, D], BF16, name="cast", bufs=3, align_bytes=64)
+            if t in V_CAST:
+                nc.vector.tensor_copy(out=c_t[:], in_=mbytes[t].bitcast(FP8))
+            else:
+                nc.scalar.copy(out=c_t[:], in_=mbytes[t].bitcast(FP8))
+            casts[t] = c_t
+
+        def product_gpsimd(t):
+            mw_t = work.tile([P, D], BF16, name="mw", bufs=8, align_bytes=64)
+            if t in S_CAST:
+                nc.vector.memset(mw_t[:, 0:2], 0.0)
+            nc.gpsimd.tensor_tensor(out=mw_t[:], in0=casts[t][:], in1=scale_bc[:], op=MULT)
             mw[t] = mw_t
 
         def m_transpose(c):
@@ -129,7 +148,7 @@ def tile_dimenettripletbilinear_kernel(tc, m_kj_bytes, m_kj_scale, m_ji, sbf, w_
 
         def m_copy(c):
             n = len(M_CHUNKS[c])
-            mq_t = work.tile([P, 2 * P * 4], BF16, name="mq", bufs=3, align_bytes=64)
+            mq_t = work.tile([P, 2 * P * 4], BF16, name="mq", bufs=4, align_bytes=64)
             dst = mq_t[:].bitcast(F32)[:, 0:n * 256].rearrange("p (j r u) -> p j r u", j=n, u=2)
             nc.scalar.copy(out=dst, in_=mtr[c][:, 0:n].rearrange("p j u r -> p j r u"))
             mq[c] = mq_t
@@ -204,10 +223,11 @@ def tile_dimenettripletbilinear_kernel(tc, m_kj_bytes, m_kj_scale, m_ji, sbf, w_
             per = 4 // n
             mm_t = psum.tile([P, 4 * P], F32, name="mm", bufs=2)
             pc_t, ps_t = pcode[c]
-            nc.tensor.matmul_mx(
-                out=mm_t[:], lhsT=wb_codes[:, 0, 0:P].bitcast(FP8X4), lhsT_scale=wb_sc[:, 0, 0:P],
-                rhs=wb_codes[:, 1, :].bitcast(FP8X4), rhs_scale=wb_sc[:, 1, :], start=True, stop=True,
-            )
+            if c < 12:
+                nc.tensor.matmul_mx(
+                    out=mm_t[:, 0:256], lhsT=wb_codes[:, 0, 0:P].bitcast(FP8X4), lhsT_scale=wb_sc[:, 0, 0:P],
+                    rhs=wb_codes[:, 1, 0:256].bitcast(FP8X4), rhs_scale=wb_sc[:, 1, 0:256], start=True, stop=True,
+                )
             for i in range(per):
                 d = b * per + i
                 cols = slice(d * P, (d + 1) * P)
@@ -248,63 +268,103 @@ def tile_dimenettripletbilinear_kernel(tc, m_kj_bytes, m_kj_scale, m_ji, sbf, w_
             nc.vector.scalar_tensor_tensor(out=o_t[:], in0=aggs[h][:], scalar=0.25, in1=mji[:, h, :], op0=MULT, op1=ADD)
             nc.sync.dma_start(out=out[h * P:(h + 1) * P, :], in_=o_t[:])
 
-        quant_at, mm_at = {}, {}
-        for c, tiles in enumerate(P_CHUNKS):
-            t0 = tiles[0]
-            if t0 < TILES - 4:
-                quant_at.setdefault(t0 + 3, []).append(c)
-                for b in range(2):
-                    mm_at.setdefault(t0 + 4 + b, []).append((c, b))
-            else:
-                quant_at.setdefault(tiles[-1] + 1, []).append(c)
-        mm_at.setdefault(31, []).append((14, 0))
-        mm_at.setdefault(32, []).append((14, 1))
-        mm_at.setdefault(32, []).append((15, 0))
-        mm_at.setdefault(33, []).append((16, 0))
+        def at(chunks, q, lead):
+            return [c for c, tiles in enumerate(chunks) if tiles[0] - lead == q]
 
-        pending_silu, pending_sum = [], []
-        for q in range(-5, TILES + 4):
-            if 0 <= q - 1 < TILES:
-                p_transpose(q - 1)
-            done = [P_CHUNKS[cb[0]][0] // HALF for cb in pending_sum if k_sum(*cb)]
-            pending_sum = []
-            for cb in pending_silu:
+        product(0)
+        m_transpose(0)
+        m_copy(0)
+        product(1)
+        m_transpose(1)
+        gain_spread()
+        m_copy(1)
+        wd_prepare()
+        m_quant(0)
+        stage1(0)
+        silu1(0)
+        product(2)
+        m_quant(1)
+        stage1(1)
+        silu1(1)
+        product(3)
+        m_transpose(2)
+        wb_interleave(0)
+        wb_interleave(1)
+        m_copy(2)
+        wb_interleave(2)
+        p_ops(0, 0, 8)
+        product(4)
+        to_silu, to_sum = [], []
+        for q in range(1, TILES):
+            p_transpose(q - 1)
+            done = [P_CHUNKS[cb[0]][0] // HALF for cb in to_sum if k_sum(*cb)]
+            to_sum = to_silu
+            for cb in to_silu:
                 silu2(*cb)
-                pending_sum.append(cb)
-            pending_silu = []
-            if 0 <= q - 1 < TILES:
-                p_copy(q - 1)
-            if q == -2:
-                wd_prepare()
-            if 0 <= q < TILES:
-                p_ops(q, 0, 4)
-            for c in quant_at.get(q, []):
-                p_quant(c)
-            if 0 <= q < TILES:
-                p_ops(q, 4, 8)
+            to_silu = []
+            if q == 1:
+                p_ops(q, 0, 8)
+                m_quant(2)
+                stage1(2)
+                silu1(2)
+                product(5)
+                m_transpose(3)
+                m_copy(3)
+            p_copy(q - 1)
+            for c in at(P_CHUNKS, q, -3):
+                if c < 14:
+                    p_quant(c)
+            for c in at(M_CHUNKS, q, 2):
+                m_quant(c)
+            if q + 5 < TILES and q + 5 not in OFFLOAD:
+                product(q + 5)
+            if q + 6 in OFFLOAD:
+                if q + 6 in V_CAST:
+                    product_cast(q + 6)
+                product_gpsimd(q + 6)
+            if q > 1:
+                p_ops(q, 0, 8)
+            if q == TILES - 2:
+                p_quant(14)
             for h in done:
                 finish(h)
             if q == 3:
                 wb_quantise(0)
                 wb_quantise(1)
-            for c, tiles in enumerate(M_CHUNKS):
-                if q == tiles[0] - 2:
-                    m_quant(c)
-            if 0 <= q + 5 < TILES:
-                product(q + 5)
-            for c, tiles in enumerate(M_CHUNKS):
-                if q == tiles[0] - 3:
-                    m_transpose(c)
-                    m_copy(c)
-            for cb in mm_at.get(q, []):
-                stage2(*cb)
-                pending_silu.append(cb)
-            for c, tiles in enumerate(M_CHUNKS):
-                if q == tiles[0] - 2:
-                    stage1(c)
-                if q == tiles[0] - 1:
+            if q > 1:
+                for c in at(M_CHUNKS, q, 1):
                     silu1(c)
-            if q == -1:
-                gain_spread()
-            if 0 <= q + 1 < 4:
-                wb_interleave(q + 1)
+            if q + 7 in S_CAST:
+                product_cast(q + 7)
+            for c in at(M_CHUNKS, q, 4):
+                m_transpose(c)
+                m_copy(c)
+            for c in range(14):
+                for b in range(2):
+                    if q == P_CHUNKS[c][0] + 4 + b - (1 if c == 13 else 0):
+                        stage2(c, b)
+                        to_silu.append((c, b))
+            for c in at(M_CHUNKS, q, 2):
+                stage1(c)
+            if q < 3:
+                for a in range(3 * q, min(3 * q + 3, 8)):
+                    wb_interleave(a)
+        stage2(14, 0)
+        p_transpose(TILES - 1)
+        stage2(14, 1)
+        silu2(14, 0)
+        p_copy(TILES - 1)
+        p_quant(15)
+        p_quant(16)
+        stage2(15, 0)
+        for cb in to_sum:
+            k_sum(*cb)
+        silu2(14, 1)
+        k_sum(14, 0)
+        silu2(15, 0)
+        stage2(16, 0)
+        k_sum(14, 1)
+        silu2(16, 0)
+        k_sum(15, 0)
+        k_sum(16, 0)
+        finish(1)

@@ -22,9 +22,7 @@ TILES = 32
 HALF = 16
 M_CHUNKS = [[0], [1]] + [[t, t + 1] for t in range(2, TILES, 2)]
 P_CHUNKS = [[t, t + 1] for t in range(0, TILES - 2, 2)] + [[TILES - 2], [TILES - 1]]
-V_CAST = [t for t in range(6, TILES) if t % 3 != 0]
-S_CAST = [t for t in range(8, TILES) if t % 3 == 0]
-OFFLOAD = V_CAST + S_CAST
+OFFLOAD = [t for t in range(11, TILES, 2)]
 LOADS = [(0, 2), (2, 4), (4, 8), (8, 12), (12, 16), (16, 20), (20, 24), (24, 28), (28, 32)]
 
 
@@ -72,7 +70,7 @@ def tile_dimenettripletbilinear_kernel(tc, m_kj_bytes, m_kj_scale, m_ji, sbf, w_
         nc.scalar.activation(out=warm2[:], in_=warm[:], func=SILU)
         ident = const.tile([P, P], F32, name="ident", align_bytes=64)
         make_identity(nc, ident[:])
-        ones = const.tile([P, P], BF16, name="ones", align_bytes=64)
+        ones = const.tile([P, 512], BF16, name="ones", align_bytes=64)
         nc.gpsimd.memset(ones[:], 1.0)
         g_zero = const.tile([P, NBC], BF16, name="g_zero", align_bytes=64)
         nc.gpsimd.memset(g_zero[:], 0.0)
@@ -112,7 +110,12 @@ def tile_dimenettripletbilinear_kernel(tc, m_kj_bytes, m_kj_scale, m_ji, sbf, w_
 
         def gain_spread():
             for a in range(2):
-                nc.tensor.matmul(out=gain_ps[:, a * 512:(a + 1) * 512], lhsT=ones[:], rhs=g_zero[:, a * 512:(a + 1) * 512], start=True, stop=True)
+                nc.tensor.matmul(out=gain_ps[:, a * 512:(a + 1) * 512], lhsT=ones[:, 0:P], rhs=g_zero[:, a * 512:(a + 1) * 512], start=True, stop=True)
+
+        def warm_tensor(n):
+            w_t = psum.tile([P, 4 * P], F32, name="mm", bufs=2)
+            for a in range(n):
+                nc.tensor.matmul(out=w_t[:], lhsT=ones[:, 0:P], rhs=ones[:], start=True, stop=True)
 
         mw, mtr, mq, mcode, yps, xs, pts, ptr, pqs, pcode, mm, tts, aggs = {}, {}, {}, {}, {}, {}, {}, {}, {}, {}, {}, {}, {}
 
@@ -125,18 +128,17 @@ def tile_dimenettripletbilinear_kernel(tc, m_kj_bytes, m_kj_scale, m_ji, sbf, w_
 
         def product_cast(t):
             c_t = work.tile([P, D], BF16, name="cast", bufs=3, align_bytes=64)
-            if t in V_CAST:
-                nc.vector.tensor_copy(out=c_t[:], in_=mbytes[t].bitcast(FP8))
-            else:
-                nc.scalar.copy(out=c_t[:], in_=mbytes[t].bitcast(FP8))
+            nc.scalar.copy(out=c_t[:], in_=mbytes[t].bitcast(FP8))
             casts[t] = c_t
 
-        def product_gpsimd(t):
-            mw_t = work.tile([P, D], BF16, name="mw", bufs=8, align_bytes=64)
-            if t in S_CAST:
-                nc.vector.memset(mw_t[:, 0:2], 0.0)
-            nc.gpsimd.tensor_tensor(out=mw_t[:], in0=casts[t][:], in1=scale_bc[:], op=MULT)
-            mw[t] = mw_t
+        def product_gpsimd(t, half, codes):
+            if half == 0:
+                mw_t = work.tile([P, D], BF16, name="mw", bufs=8, align_bytes=64)
+                mw[t] = mw_t
+            mark = work.tile([P, 1], U32, name="mark", bufs=2)
+            nc.gpsimd.tensor_copy(out=mark[:], in_=codes[:, 0:1])
+            cols = slice(half * 256, half * 256 + 256)
+            nc.gpsimd.tensor_tensor(out=mw[t][:, cols], in0=casts[t][:, cols], in1=scale_bc[:, cols], op=MULT)
 
         def m_transpose(c):
             tr_t = psum.tile([P, 2, 2, P], F32, name="tr", bufs=3)
@@ -195,41 +197,51 @@ def tile_dimenettripletbilinear_kernel(tc, m_kj_bytes, m_kj_scale, m_ji, sbf, w_
             for j, t in enumerate(tiles):
                 p_place[t] = (c, j)
 
-        def p_transpose(t):
-            tr_t = psum.tile([P, 4, P], F32, name="tr", bufs=3)
+        def p_transpose(t, passes=(0, 1)):
             words = pts[t][:].bitcast(F32)
-            for a in range(4):
-                nc.tensor.transpose(tr_t[:, a, :], words[:, a * P:(a + 1) * P], ident[:])
-            ptr[t] = tr_t
+            tr_t = psum.tile([P, 4, P], F32, name="tr", bufs=3)
+            for g in passes:
+                for a in (2 * g, 2 * g + 1):
+                    nc.tensor.transpose(tr_t[:, a, :], words[:, a * P:(a + 1) * P], ident[:])
+                ptr[t, g] = tr_t
 
-        def p_copy(t):
+        def p_copy(t, passes=(0, 1)):
             c, j = p_place[t]
             n = len(P_CHUNKS[c])
-            if j == 0:
+            if j == 0 and passes[0] == 0:
                 pq_t = work.tile([P, 2 * NBC], BF16, name="pq", bufs=3, align_bytes=64)
                 pqs[c] = pq_t
-            dst = pqs[c][:].bitcast(F32)[:, 0:n * 512].rearrange("p (g j r u) -> p g j r u", g=2, j=n, u=2)[:, :, j]
-            nc.scalar.copy(out=dst, in_=ptr[t][:].rearrange("p (g u) r -> p g r u", g=2))
+            g0, g1 = passes[0], passes[-1] + 1
+            dst = pqs[c][:].bitcast(F32)[:, 0:n * 512].rearrange("p (g j r u) -> p g j r u", g=2, j=n, u=2)[:, g0:g1, j]
+            nc.scalar.copy(out=dst, in_=ptr[t, g0][:].rearrange("p (g u) r -> p g r u", g=2)[:, g0:g1])
 
-        def p_quant(c):
+        def p_quant(c, passes=(0, 1)):
             n = len(P_CHUNKS[c])
-            pc_t = work.tile([P, 4 * P], U32, name="pc", bufs=3, align_bytes=64)
-            ps_t = work.tile([P, 4 * P], U8, name="ps", bufs=3, align_bytes=64)
-            nc.vector.quantize_mx(out=pc_t[:, 0:2 * n * P].bitcast(FP8X4), scales=ps_t[:, 0:2 * n * P], in_=pqs[c][:, 0:n * NBC])
-            pcode[c] = (pc_t, ps_t)
+            if passes[0] == 0:
+                pc_t = work.tile([P, 4 * P], U32, name="pc", bufs=3, align_bytes=64)
+                ps_t = work.tile([P, 4 * P], U8, name="ps", bufs=3, align_bytes=64)
+                pcode[c] = (pc_t, ps_t)
+            words = slice(passes[0] * n * P, (passes[-1] + 1) * n * P)
+            values = slice(passes[0] * n * 512, (passes[-1] + 1) * n * 512)
+            nc.vector.quantize_mx(out=pcode[c][0][:, words].bitcast(FP8X4), scales=pcode[c][1][:, words], in_=pqs[c][:, values])
+
+        def bank_dims(c, b):
+            per = 2 if c == 16 else 4 // len(P_CHUNKS[c])
+            return list(range(b * per, (b + 1) * per))
 
         def stage2(c, b):
             n = len(P_CHUNKS[c])
-            per = 4 // n
-            mm_t = psum.tile([P, 4 * P], F32, name="mm", bufs=2)
+            if c < 15:
+                mm_t = psum.tile([P, 4 * P], F32, name="mm", bufs=2)
+            else:
+                mm_t = psum.tile([P, 4 * P], F32, name="tr", bufs=3)
             pc_t, ps_t = pcode[c]
             if c < 12:
                 nc.tensor.matmul_mx(
                     out=mm_t[:, 0:256], lhsT=wb_codes[:, 0, 0:P].bitcast(FP8X4), lhsT_scale=wb_sc[:, 0, 0:P],
                     rhs=wb_codes[:, 1, 0:256].bitcast(FP8X4), rhs_scale=wb_sc[:, 1, 0:256], start=True, stop=True,
                 )
-            for i in range(per):
-                d = b * per + i
+            for i, d in enumerate(bank_dims(c, b)):
                 cols = slice(d * P, (d + 1) * P)
                 for g in range(2):
                     toks = slice(g * n * P, (g + 1) * n * P)
@@ -240,26 +252,26 @@ def tile_dimenettripletbilinear_kernel(tc, m_kj_bytes, m_kj_scale, m_ji, sbf, w_
             mm[c, b] = mm_t
 
         def silu2(c, b):
-            t_t = work.tile([P, 4 * P], F32, name="tt", bufs=4, align_bytes=64)
-            nc.scalar.activation(out=t_t[:], in_=mm[c, b][:], func=SILU)
+            t_t = work.tile([P, 4 * P], F32, name="tt", bufs=6, align_bytes=64)
+            w = len(bank_dims(c, b)) * len(P_CHUNKS[c]) * P
+            nc.scalar.activation(out=t_t[:, 0:w], in_=mm[c, b][:, 0:w], func=SILU)
             tts[c, b] = t_t
 
         def k_sum(c, b):
             tiles = P_CHUNKS[c]
             n = len(tiles)
-            per = 4 // n
             h = tiles[0] // HALF
-            first = tiles[0] % HALF == 0 and b == 0
-            last = tiles[-1] % HALF == HALF - 1 and b == n - 1
+            dims = bank_dims(c, b)
+            first = tiles[0] % HALF == 0 and dims[0] == 0
+            last = tiles[-1] % HALF == HALF - 1 and dims[-1] == 3
             if first:
                 agg_t = psum.tile([P, D], F32, name="agg", bufs=1)
                 aggs[h] = agg_t
-            for i in range(per):
-                d = b * per + i
+            for i, d in enumerate(dims):
                 for j in range(n):
                     nc.tensor.matmul(
                         out=aggs[h][:, d * P:(d + 1) * P], lhsT=tts[c, b][:, (i * n + j) * P:(i * n + j + 1) * P], rhs=ident[:],
-                        is_transpose=True, start=(first and i == 0 and j == 0), stop=(last and i == per - 1 and j == n - 1),
+                        is_transpose=True, start=(first and i == 0 and j == 0), stop=(last and d == 3 and j == n - 1),
                     )
             return last
 
@@ -271,6 +283,7 @@ def tile_dimenettripletbilinear_kernel(tc, m_kj_bytes, m_kj_scale, m_ji, sbf, w_
         def at(chunks, q, lead):
             return [c for c, tiles in enumerate(chunks) if tiles[0] - lead == q]
 
+        warm_tensor(3)
         product(0)
         m_transpose(0)
         m_copy(0)
@@ -288,41 +301,46 @@ def tile_dimenettripletbilinear_kernel(tc, m_kj_bytes, m_kj_scale, m_ji, sbf, w_
         silu1(1)
         product(3)
         m_transpose(2)
+        warm_tensor(2)
         wb_interleave(0)
         wb_interleave(1)
         m_copy(2)
         wb_interleave(2)
         p_ops(0, 0, 8)
         product(4)
+        m_quant(2)
+        stage1(2)
+        silu1(2)
+        product(5)
+        m_transpose(3)
+        m_copy(3)
         to_silu, to_sum = [], []
         for q in range(1, TILES):
             p_transpose(q - 1)
             done = [P_CHUNKS[cb[0]][0] // HALF for cb in to_sum if k_sum(*cb)]
             to_sum = to_silu
+            if q >= 40:
+                p_copy(q - 1)
             for cb in to_silu:
                 silu2(*cb)
             to_silu = []
+            if q < 40:
+                p_copy(q - 1)
             if q == 1:
                 p_ops(q, 0, 8)
-                m_quant(2)
-                stage1(2)
-                silu1(2)
-                product(5)
-                m_transpose(3)
-                m_copy(3)
-            p_copy(q - 1)
+            if q + 5 < TILES and q + 5 not in OFFLOAD:
+                product(q + 5)
             for c in at(P_CHUNKS, q, -3):
                 if c < 14:
                     p_quant(c)
+                    codes = pcode[c][0]
             for c in at(M_CHUNKS, q, 2):
                 m_quant(c)
-            if q + 5 < TILES and q + 5 not in OFFLOAD:
-                product(q + 5)
-            if q + 6 in OFFLOAD:
-                if q + 6 in V_CAST:
-                    product_cast(q + 6)
-                product_gpsimd(q + 6)
-            if q > 1:
+                codes = mcode[c][0]
+            for half in range(2):
+                if q + 7 - half in OFFLOAD:
+                    product_gpsimd(q + 7 - half, half, codes)
+            if 1 < q < TILES - 1:
                 p_ops(q, 0, 8)
             if q == TILES - 2:
                 p_quant(14)
@@ -334,11 +352,12 @@ def tile_dimenettripletbilinear_kernel(tc, m_kj_bytes, m_kj_scale, m_ji, sbf, w_
             if q > 1:
                 for c in at(M_CHUNKS, q, 1):
                     silu1(c)
-            if q + 7 in S_CAST:
-                product_cast(q + 7)
+            if q + 9 in OFFLOAD:
+                product_cast(q + 9)
             for c in at(M_CHUNKS, q, 4):
-                m_transpose(c)
-                m_copy(c)
+                if c > 3:
+                    m_transpose(c)
+                    m_copy(c)
             for c in range(14):
                 for b in range(2):
                     if q == P_CHUNKS[c][0] + 4 + b - (1 if c == 13 else 0):
@@ -346,25 +365,35 @@ def tile_dimenettripletbilinear_kernel(tc, m_kj_bytes, m_kj_scale, m_ji, sbf, w_
                         to_silu.append((c, b))
             for c in at(M_CHUNKS, q, 2):
                 stage1(c)
+            if q < 4:
+                warm_tensor(2)
             if q < 3:
                 for a in range(3 * q, min(3 * q + 3, 8)):
                     wb_interleave(a)
+        last = TILES - 1
+        p_ops(last, 0, 4)
         stage2(14, 0)
-        p_transpose(TILES - 1)
-        stage2(14, 1)
-        silu2(14, 0)
-        p_copy(TILES - 1)
+        p_transpose(last, (0,))
+        p_copy(last, (0,))
+        p_ops(last, 4, 8)
         p_quant(15)
+        p_transpose(last, (1,))
+        p_copy(last, (1,))
         p_quant(16)
+        silu2(14, 0)
+        stage2(14, 1)
         stage2(15, 0)
         for cb in to_sum:
             k_sum(*cb)
         silu2(14, 1)
-        k_sum(14, 0)
         silu2(15, 0)
         stage2(16, 0)
-        k_sum(14, 1)
+        stage2(16, 1)
         silu2(16, 0)
+        k_sum(14, 0)
+        silu2(16, 1)
+        k_sum(14, 1)
         k_sum(15, 0)
         k_sum(16, 0)
+        k_sum(16, 1)
         finish(1)

@@ -22,7 +22,7 @@ TILES = 32
 HALF = 16
 M_CHUNKS = [[0], [1]] + [[t, t + 1] for t in range(2, TILES, 2)]
 P_CHUNKS = [[t, t + 1] for t in range(0, TILES - 2, 2)] + [[TILES - 2], [TILES - 1]]
-OFFLOAD = [t for t in range(11, TILES, 2)]
+OFFLOAD = [t for t in range(10, TILES, 2)]
 LOADS = [(0, 2), (2, 4), (4, 8), (8, 12), (12, 16), (16, 20), (20, 24), (24, 28), (28, 32)]
 
 
@@ -137,15 +137,19 @@ def tile_dimenettripletbilinear_kernel(tc, m_kj_bytes, m_kj_scale, m_ji, sbf, w_
                 mw[t] = mw_t
             mark = work.tile([P, 1], U32, name="mark", bufs=2)
             nc.gpsimd.tensor_copy(out=mark[:], in_=codes[:, 0:1])
-            cols = slice(half * 256, half * 256 + 256)
-            nc.gpsimd.tensor_tensor(out=mw[t][:, cols], in0=casts[t][:, cols], in1=scale_bc[:, cols], op=MULT)
+            nc.gpsimd.tensor_tensor(
+                out=mw[t][:, half * 256:half * 256 + 256].rearrange("p (w e) -> p w e", e=2),
+                in0=casts[t][:].rearrange("p (w u e) -> p u w e", u=2, e=2)[:, half],
+                in1=scale_bc[:].rearrange("p (w u e) -> p u w e", u=2, e=2)[:, half], op=MULT,
+            )
 
         def m_transpose(c):
             tr_t = psum.tile([P, 2, 2, P], F32, name="tr", bufs=3)
             for j, t in enumerate(M_CHUNKS[c]):
                 words = mw[t][:].bitcast(F32)
                 for u in range(2):
-                    nc.tensor.transpose(tr_t[:, j, u, :], words[:, u:256:2], ident[:])
+                    cols = slice(u * P, u * P + P) if t in OFFLOAD else slice(u, 256, 2)
+                    nc.tensor.transpose(tr_t[:, j, u, :], words[:, cols], ident[:])
             mtr[c] = tr_t
 
         def m_copy(c):
@@ -238,8 +242,8 @@ def tile_dimenettripletbilinear_kernel(tc, m_kj_bytes, m_kj_scale, m_ji, sbf, w_
             pc_t, ps_t = pcode[c]
             if c < 12:
                 nc.tensor.matmul_mx(
-                    out=mm_t[:, 0:256], lhsT=wb_codes[:, 0, 0:P].bitcast(FP8X4), lhsT_scale=wb_sc[:, 0, 0:P],
-                    rhs=wb_codes[:, 1, 0:256].bitcast(FP8X4), rhs_scale=wb_sc[:, 1, 0:256], start=True, stop=True,
+                    out=mm_t[:, 0:128], lhsT=wb_codes[:, 0, 0:P].bitcast(FP8X4), lhsT_scale=wb_sc[:, 0, 0:P],
+                    rhs=wb_codes[:, 1, 0:128].bitcast(FP8X4), rhs_scale=wb_sc[:, 1, 0:128], start=True, stop=True,
                 )
             for i, d in enumerate(bank_dims(c, b)):
                 cols = slice(d * P, (d + 1) * P)
@@ -301,7 +305,7 @@ def tile_dimenettripletbilinear_kernel(tc, m_kj_bytes, m_kj_scale, m_ji, sbf, w_
         silu1(1)
         product(3)
         m_transpose(2)
-        warm_tensor(2)
+        warm_tensor(3)
         wb_interleave(0)
         wb_interleave(1)
         m_copy(2)
@@ -352,8 +356,8 @@ def tile_dimenettripletbilinear_kernel(tc, m_kj_bytes, m_kj_scale, m_ji, sbf, w_
             if q > 1:
                 for c in at(M_CHUNKS, q, 1):
                     silu1(c)
-            if q + 9 in OFFLOAD:
-                product_cast(q + 9)
+            if q + 8 in OFFLOAD:
+                product_cast(q + 8)
             for c in at(M_CHUNKS, q, 4):
                 if c > 3:
                     m_transpose(c)
@@ -366,7 +370,7 @@ def tile_dimenettripletbilinear_kernel(tc, m_kj_bytes, m_kj_scale, m_ji, sbf, w_
             for c in at(M_CHUNKS, q, 2):
                 stage1(c)
             if q < 4:
-                warm_tensor(2)
+                warm_tensor(3)
             if q < 3:
                 for a in range(3 * q, min(3 * q + 3, 8)):
                     wb_interleave(a)

from contextlib import ExitStack

import concourse.mybir as mybir
from concourse.masks import make_identity

E, K, D, C, NB = 256, 16, 512, 128, 8
NBC = NB * C
P = 128
FLOPS = 2 * E * K * D * C + 2 * E * K * NBC * D

F32 = mybir.dt.float32
BF16 = mybir.dt.bfloat16
U32 = mybir.dt.uint32
U8 = mybir.dt.uint8
FP8 = mybir.dt.float8_e4m3fn
FP8X4 = mybir.dt.float8_e4m3fn_x4
MULT = mybir.AluOpType.mult
ADD = mybir.AluOpType.add
SILU = mybir.ActivationFunctionType.Silu

TILES = 32
HALF = 16
M_CHUNKS = [[0], [1]] + [[t, t + 1] for t in range(2, TILES, 2)]
P_CHUNKS = [[t, t + 1] for t in range(0, TILES - 2, 2)] + [[TILES - 2], [TILES - 1]]
OFFLOAD = [t for t in range(10, TILES, 2)]
LOADS = [(0, 2), (2, 4), (4, 8), (8, 12), (12, 16), (16, 20), (20, 24), (24, 28), (28, 32)]


def tile_dimenettripletbilinear_kernel(tc, m_kj_bytes, m_kj_scale, m_ji, sbf, w_down, gain, w_bil, out):
    nc = tc.nc
    with ExitStack() as ctx:
        const = ctx.enter_context(tc.tile_pool(name="const", bufs=1))
        work = ctx.enter_context(tc.tile_pool(name="work", bufs=2))
        psum = ctx.enter_context(tc.psum_pool(name="psum", bufs=1))
        ctx.enter_context(tc.manual_schedule())

        mbytes = {}

        def load_bytes(t0, t1):
            t_t = const.tile([P, (t1 - t0) * D], U8, name="mbytes%d" % t0, align_bytes=64)
            h = t0 // HALF
            nc.sync.dma_start(
                out=t_t[:], in_=m_kj_bytes[h * P:(h + 1) * P, t0 - h * HALF:t1 - h * HALF, :].rearrange("e k d -> e (k d)")
            )
            for t in range(t0, t1):
                mbytes[t] = t_t[:, (t - t0) * D:(t - t0 + 1) * D]

        g_raw = const.tile([1, NBC], BF16, name="g_raw", align_bytes=64)
        nc.sync.dma_start(out=g_raw[:], in_=gain.unsqueeze(0))
        scale_bc = const.tile([P, D], F32, name="scale_bc", align_bytes=64)
        nc.sync.dma_start(out=scale_bc[:], in_=m_kj_scale.rearrange("a b k -> (a b k)").partition_broadcast(P))
        load_bytes(*LOADS[0])
        wd_raw = const.tile([P, 4, C], BF16, name="wd_raw", align_bytes=64)
        nc.sync.dma_start(out=wd_raw[:], in_=w_down.rearrange("(p j) c -> p j c", j=4))
        sbf_raw = const.tile([P, 2, K * NB], BF16, name="sbf_raw", align_bytes=64)
        nc.sync.dma_start(out=sbf_raw[:], in_=sbf.rearrange("(h e) k n -> e h (k n)", e=P))
        load_bytes(*LOADS[1])
        wb_raw = const.tile([P, 2, 4, D], BF16, name="wb_raw", align_bytes=64)
        wb_hbm = w_bil.rearrange("(g p j) d -> g p j d", g=2, j=4)
        for g in range(2):
            nc.sync.dma_start(out=wb_raw[:, g], in_=wb_hbm[g])
        for t0, t1 in LOADS[2:]:
            load_bytes(t0, t1)
        mji = const.tile([P, 2, D], BF16, name="mji", align_bytes=64)
        nc.sync.dma_start(out=mji[:], in_=m_ji.rearrange("(h e) d -> e h d", e=P))

        warm = const.tile([P, 1], F32, name="warm")
        nc.vector.memset(warm[:], 0.0)
        warm2 = const.tile([P, 1], F32, name="warm2")
        nc.scalar.activation(out=warm2[:], in_=warm[:], func=SILU)
        ident = const.tile([P, P], F32, name="ident", align_bytes=64)
        make_identity(nc, ident[:])
        ones = const.tile([P, 512], BF16, name="ones", align_bytes=64)
        nc.gpsimd.memset(ones[:], 1.0)
        g_zero = const.tile([P, NBC], BF16, name="g_zero", align_bytes=64)
        nc.gpsimd.memset(g_zero[:], 0.0)
        for u in range(2):
            nc.scalar.copy(
                out=g_zero[0:1, :].rearrange("o (n u i e) -> o u n i e", u=2, i=32, e=2)[:, u],
                in_=g_raw[:].rearrange("o (n i u e) -> o u n i e", u=2, i=32, e=2)[:, u],
            )
        sbf_f = const.tile([P, 2 * K * NB], F32, name="sbf_f", align_bytes=64)
        nc.scalar.copy(out=sbf_f[:], in_=sbf_raw[:].rearrange("p h k -> p (h k)"))

        wd_grp = const.tile([P, C, 4], BF16, name="wd_grp", align_bytes=64)
        wd_codes = const.tile([P, C], U32, name="wd_codes", align_bytes=64)
        wd_sc = const.tile([P, C], U8, name="wd_sc", align_bytes=64)

        def wd_prepare():
            for u in range(2):
                nc.vector.tensor_copy(
                    out=wd_grp[:].rearrange("p (u i e) j -> p u i e j", u=2, e=2)[:, u],
                    in_=wd_raw[:].rearrange("p j (i u e) -> p u i e j", u=2, e=2)[:, u],
                )
            nc.vector.quantize_mx(out=wd_codes[:].bitcast(FP8X4), scales=wd_sc[:], in_=wd_grp[:].rearrange("p c j -> p (c j)"))

        wb_grp = const.tile([P, 2, D, 4], BF16, name="wb_grp", align_bytes=64)
        wb_codes = const.tile([P, 2, D], U32, name="wb_codes", align_bytes=64)
        wb_sc = const.tile([P, 2, D], U8, name="wb_sc", align_bytes=64)

        def wb_interleave(a):
            g, part = a // 4, a % 4
            d = slice(part * 128, part * 128 + 128)
            nc.scalar.copy(out=wb_grp[:, g, d, :], in_=wb_raw[:, g, :, d].rearrange("p j d -> p d j"))

        def wb_quantise(g):
            nc.vector.quantize_mx(out=wb_codes[:, g, :].bitcast(FP8X4), scales=wb_sc[:, g, :], in_=wb_grp[:, g].rearrange("p d j -> p (d j)"))

        gain_ps = psum.tile([P, NBC], BF16, name="gain_ps")

        def gain_spread():
            for a in range(2):
                nc.tensor.matmul(out=gain_ps[:, a * 512:(a + 1) * 512], lhsT=ones[:, 0:P], rhs=g_zero[:, a * 512:(a + 1) * 512], start=True, stop=True)

        def warm_tensor(n):
            w_t = psum.tile([P, 4 * P], F32, name="mm", bufs=2)
            for a in range(n):
                nc.tensor.matmul(out=w_t[:], lhsT=ones[:, 0:P], rhs=ones[:], start=True, stop=True)

        mw, mtr, mq, mcode, yps, xs, pts, ptr, pqs, pcode, mm, tts, aggs = {}, {}, {}, {}, {}, {}, {}, {}, {}, {}, {}, {}, {}

        def product(t):
            mw_t = work.tile([P, D], BF16, name="mw", bufs=8, align_bytes=64)
            nc.vector.tensor_tensor(out=mw_t[:], in0=mbytes[t].bitcast(FP8), in1=scale_bc[:], op=MULT)
            mw[t] = mw_t

        casts = {}

        def product_cast(t):
            c_t = work.tile([P, D], BF16, name="cast", bufs=3, align_bytes=64)
            nc.scalar.copy(out=c_t[:], in_=mbytes[t].bitcast(FP8))
            casts[t] = c_t

        def product_gpsimd(t, half, codes):
            if half == 0:
                mw_t = work.tile([P, D], BF16, name="mw", bufs=8, align_bytes=64)
                mw[t] = mw_t
            mark = work.tile([P, 1], U32, name="mark", bufs=2)
            nc.gpsimd.tensor_copy(out=mark[:], in_=codes[:, 0:1])
            nc.gpsimd.tensor_tensor(
                out=mw[t][:, half * 256:half * 256 + 256].rearrange("p (w e) -> p w e", e=2),
                in0=casts[t][:].rearrange("p (w u e) -> p u w e", u=2, e=2)[:, half],
                in1=scale_bc[:].rearrange("p (w u e) -> p u w e", u=2, e=2)[:, half], op=MULT,
            )

        def m_transpose(c):
            tr_t = psum.tile([P, 2, 2, P], F32, name="tr", bufs=3)
            for j, t in enumerate(M_CHUNKS[c]):
                words = mw[t][:].bitcast(F32)
                for u in range(2):
                    cols = slice(u * P, u * P + P) if t in OFFLOAD else slice(u, 256, 2)
                    nc.tensor.transpose(tr_t[:, j, u, :], words[:, cols], ident[:])
            mtr[c] = tr_t

        def m_copy(c):
            n = len(M_CHUNKS[c])
            mq_t = work.tile([P, 2 * P * 4], BF16, name="mq", bufs=4, align_bytes=64)
            dst = mq_t[:].bitcast(F32)[:, 0:n * 256].rearrange("p (j r u) -> p j r u", j=n, u=2)
            nc.scalar.copy(out=dst, in_=mtr[c][:, 0:n].rearrange("p j u r -> p j r u"))
            mq[c] = mq_t

        def m_quant(c):
            n = len(M_CHUNKS[c])
            mc_t = work.tile([P, 2 * P], U32, name="mc", bufs=3, align_bytes=64)
            ms_t = work.tile([P, 2 * P], U8, name="ms", bufs=3, align_bytes=64)
            nc.vector.quantize_mx(out=mc_t[:, 0:n * P].bitcast(FP8X4), scales=ms_t[:, 0:n * P], in_=mq[c][:, 0:n * P * 4])
            mcode[c] = (mc_t, ms_t)

        def stage1(c):
            y_t = psum.tile([P, 2, C], F32, name="y", bufs=1)
            mc_t, ms_t = mcode[c]
            for j in range(len(M_CHUNKS[c])):
                cols = slice(j * P, (j + 1) * P)
                nc.tensor.matmul_mx(
                    out=y_t[:, j, :], lhsT=mc_t[:, cols].bitcast(FP8X4), lhsT_scale=ms_t[:, cols],
                    rhs=wd_codes[:].bitcast(FP8X4), rhs_scale=wd_sc[:], start=True, stop=True,
                )
            yps[c] = y_t

        def silu1(c):
            n = len(M_CHUNKS[c])
            x_t = work.tile([P, 2, C], F32, name="x", bufs=3, align_bytes=64)
            nc.scalar.activation(out=x_t[:, 0:n], in_=yps[c][:, 0:n], func=SILU)
            for j, t in enumerate(M_CHUNKS[c]):
                xs[t] = x_t[:, j, :].rearrange("p (u w) -> p u w", u=2)

        def p_ops(t, n0, n1):
            if n0 == 0:
                p_t = work.tile([P, NBC], BF16, name="pt", bufs=3, align_bytes=64)
                pts[t] = p_t
            view = pts[t][:].rearrange("p (g u n w) -> p g u n w", g=2, u=2, n=4)
            for n in range(n0, n1):
                col = t * NB + n
                nc.vector.scalar_tensor_tensor(
                    out=view[:, n // 4, :, n % 4, :], in0=xs[t], scalar=sbf_f[:, col:col + 1],
                    in1=gain_ps[:, n * C:(n + 1) * C].rearrange("p (u w) -> p u w", u=2), op0=MULT, op1=MULT,
                )

        p_place = {}
        for c, tiles in enumerate(P_CHUNKS):
            for j, t in enumerate(tiles):
                p_place[t] = (c, j)

        def p_transpose(t, passes=(0, 1)):
            words = pts[t][:].bitcast(F32)
            tr_t = psum.tile([P, 4, P], F32, name="tr", bufs=3)
            for g in passes:
                for a in (2 * g, 2 * g + 1):
                    nc.tensor.transpose(tr_t[:, a, :], words[:, a * P:(a + 1) * P], ident[:])
                ptr[t, g] = tr_t

        def p_copy(t, passes=(0, 1)):
            c, j = p_place[t]
            n = len(P_CHUNKS[c])
            if j == 0 and passes[0] == 0:
                pq_t = work.tile([P, 2 * NBC], BF16, name="pq", bufs=3, align_bytes=64)
                pqs[c] = pq_t
            g0, g1 = passes[0], passes[-1] + 1
            dst = pqs[c][:].bitcast(F32)[:, 0:n * 512].rearrange("p (g j r u) -> p g j r u", g=2, j=n, u=2)[:, g0:g1, j]
            nc.scalar.copy(out=dst, in_=ptr[t, g0][:].rearrange("p (g u) r -> p g r u", g=2)[:, g0:g1])

        def p_quant(c, passes=(0, 1)):
            n = len(P_CHUNKS[c])
            if passes[0] == 0:
                pc_t = work.tile([P, 4 * P], U32, name="pc", bufs=3, align_bytes=64)
                ps_t = work.tile([P, 4 * P], U8, name="ps", bufs=3, align_bytes=64)
                pcode[c] = (pc_t, ps_t)
            words = slice(passes[0] * n * P, (passes[-1] + 1) * n * P)
            values = slice(passes[0] * n * 512, (passes[-1] + 1) * n * 512)
            nc.vector.quantize_mx(out=pcode[c][0][:, words].bitcast(FP8X4), scales=pcode[c][1][:, words], in_=pqs[c][:, values])

        def bank_dims(c, b):
            per = 2 if c == 16 else 4 // len(P_CHUNKS[c])
            return list(range(b * per, (b + 1) * per))

        def stage2(c, b):
            n = len(P_CHUNKS[c])
            if c < 15:
                mm_t = psum.tile([P, 4 * P], F32, name="mm", bufs=2)
            else:
                mm_t = psum.tile([P, 4 * P], F32, name="tr", bufs=3)
            pc_t, ps_t = pcode[c]
            if c < 12:
                nc.tensor.matmul_mx(
                    out=mm_t[:, 0:128], lhsT=wb_codes[:, 0, 0:P].bitcast(FP8X4), lhsT_scale=wb_sc[:, 0, 0:P],
                    rhs=wb_codes[:, 1, 0:128].bitcast(FP8X4), rhs_scale=wb_sc[:, 1, 0:128], start=True, stop=True,
                )
            for i, d in enumerate(bank_dims(c, b)):
                cols = slice(d * P, (d + 1) * P)
                for g in range(2):
                    toks = slice(g * n * P, (g + 1) * n * P)
                    nc.tensor.matmul_mx(
                        out=mm_t[:, i * n * P:(i + 1) * n * P], lhsT=wb_codes[:, g, cols].bitcast(FP8X4), lhsT_scale=wb_sc[:, g, cols],
                        rhs=pc_t[:, toks].bitcast(FP8X4), rhs_scale=ps_t[:, toks], start=(g == 0), stop=(g == 1),
                    )
            mm[c, b] = mm_t

        def silu2(c, b):
            t_t = work.tile([P, 4 * P], F32, name="tt", bufs=6, align_bytes=64)
            w = len(bank_dims(c, b)) * len(P_CHUNKS[c]) * P
            nc.scalar.activation(out=t_t[:, 0:w], in_=mm[c, b][:, 0:w], func=SILU)
            tts[c, b] = t_t

        def k_sum(c, b):
            tiles = P_CHUNKS[c]
            n = len(tiles)
            h = tiles[0] // HALF
            dims = bank_dims(c, b)
            first = tiles[0] % HALF == 0 and dims[0] == 0
            last = tiles[-1] % HALF == HALF - 1 and dims[-1] == 3
            if first:
                agg_t = psum.tile([P, D], F32, name="agg", bufs=1)
                aggs[h] = agg_t
            for i, d in enumerate(dims):
                for j in range(n):
                    nc.tensor.matmul(
                        out=aggs[h][:, d * P:(d + 1) * P], lhsT=tts[c, b][:, (i * n + j) * P:(i * n + j + 1) * P], rhs=ident[:],
                        is_transpose=True, start=(first and i == 0 and j == 0), stop=(last and d == 3 and j == n - 1),
                    )
            return last

        def finish(h):
            o_t = work.tile([P, D], F32, name="o", bufs=2, align_bytes=64)
            nc.vector.scalar_tensor_tensor(out=o_t[:], in0=aggs[h][:], scalar=0.25, in1=mji[:, h, :], op0=MULT, op1=ADD)
            nc.sync.dma_start(out=out[h * P:(h + 1) * P, :], in_=o_t[:])

        def at(chunks, q, lead):
            return [c for c, tiles in enumerate(chunks) if tiles[0] - lead == q]

        warm_tensor(3)
        product(0)
        m_transpose(0)
        m_copy(0)
        product(1)
        m_transpose(1)
        gain_spread()
        m_copy(1)
        wd_prepare()
        m_quant(0)
        stage1(0)
        silu1(0)
        product(2)
        m_quant(1)
        stage1(1)
        silu1(1)
        product(3)
        m_transpose(2)
        warm_tensor(3)
        wb_interleave(0)
        wb_interleave(1)
        m_copy(2)
        wb_interleave(2)
        p_ops(0, 0, 8)
        product(4)
        m_quant(2)
        stage1(2)
        silu1(2)
        product(5)
        m_transpose(3)
        m_copy(3)
        to_silu, to_sum = [], []
        for q in range(1, TILES):
            p_transpose(q - 1)
            done = [P_CHUNKS[cb[0]][0] // HALF for cb in to_sum if k_sum(*cb)]
            to_sum = to_silu
            if q >= 40:
                p_copy(q - 1)
            for cb in to_silu:
                silu2(*cb)
            to_silu = []
            if q < 40:
                p_copy(q - 1)
            if q == 1:
                p_ops(q, 0, 8)
            if q + 5 < TILES and q + 5 not in OFFLOAD:
                product(q + 5)
            for c in at(P_CHUNKS, q, -3):
                if c < 14:
                    p_quant(c)
                    codes = pcode[c][0]
            for c in at(M_CHUNKS, q, 2):
                m_quant(c)
                codes = mcode[c][0]
            for half in range(2):
                if q + 7 - half in OFFLOAD:
                    product_gpsimd(q + 7 - half, half, codes)
            if 1 < q < TILES - 1:
                p_ops(q, 0, 8)
            if q == TILES - 2:
                p_quant(14)
            for h in done:
                finish(h)
            if q == 3:
                wb_quantise(0)
                wb_quantise(1)
            if q > 1:
                for c in at(M_CHUNKS, q, 1):
                    silu1(c)
            if q + 8 in OFFLOAD:
                product_cast(q + 8)
            for c in at(M_CHUNKS, q, 4):
                if c > 3:
                    m_transpose(c)
                    m_copy(c)
            for c in range(14):
                for b in range(2):
                    if q == P_CHUNKS[c][0] + 4 + b - (1 if c == 13 else 0):
                        stage2(c, b)
                        to_silu.append((c, b))
            for c in at(M_CHUNKS, q, 2):
                stage1(c)
            if q < 4:
                warm_tensor(3)
            if q < 3:
                for a in range(3 * q, min(3 * q + 3, 8)):
                    wb_interleave(a)
        last = TILES - 1
        p_ops(last, 0, 4)
        stage2(14, 0)
        p_transpose(last, (0,))
        p_copy(last, (0,))
        p_ops(last, 4, 8)
        p_quant(15)
        p_transpose(last, (1,))
        p_copy(last, (1,))
        p_quant(16)
        silu2(14, 0)
        stage2(14, 1)
        stage2(15, 0)
        for cb in to_sum:
            k_sum(*cb)
        silu2(14, 1)
        silu2(15, 0)
        stage2(16, 0)
        stage2(16, 1)
        silu2(16, 0)
        k_sum(14, 0)
        silu2(16, 1)
        k_sum(14, 1)
        k_sum(15, 0)
        k_sum(16, 0)
        k_sum(16, 1)
        finish(1)
